import numpy as np
import ml_dtypes


def mxq(x, axis, fmt="e4m3"):
    dtype, down = {"e4m3": (ml_dtypes.float8_e4m3fn, 7), "e5m2": (ml_dtypes.float8_e5m2, 14)}[fmt]
    v = np.moveaxis(np.asarray(x, np.float32).astype(ml_dtypes.bfloat16).astype(np.float64), axis, -1)
    blocks = v.reshape(v.shape[:-1] + (-1, 32))
    amax = np.abs(blocks).max(-1, keepdims=True)
    byte = np.maximum(np.where(amax > 0, np.frexp(amax)[1] - 1 + 127, 0) - down, 1)
    scale = np.exp2(byte - 127.0)
    codes = (blocks / scale).astype(np.float32).astype(dtype).astype(np.float64)
    return np.moveaxis((codes * scale).reshape(v.shape), -1, axis)


WIDE = False


def mx_kscale(k):
    if not WIDE:
        return np.ones(k)
    levels = np.array([10, -10, 5, -5, 0])
    if k % 512:
        return np.exp2(np.random.permutation(np.resize(levels, k // 32))).repeat(32)
    a = np.empty((k // 512, 16))
    for p in range(k // 512):
        a[p, :8] = np.random.permutation(np.resize(levels, 8))
        for g in range(8):
            far = levels[np.abs(levels - a[p, g]) >= 10]
            a[p, g + 8] = far[np.random.randint(len(far))]
    return np.exp2(a.ravel()).repeat(32)


def f64(x):
    return np.asarray(x).astype(np.float64)


def striped(idx):
    return np.tile(np.asarray(idx).reshape(-1, 16).T, (8, 1)).astype(np.uint16)


def unstriped(offs):
    return offs[:16].T.reshape(-1).astype(np.int64)


E2M1 = np.array([0.0, 0.5, 1.0, 1.5, 2.0, 3.0, 4.0, 6.0, -0.0, -0.5, -1.0, -1.5, -2.0, -3.0, -4.0, -6.0])


def pack_weight(w, fmt):
    k, n = w.shape
    w = f64(np.asarray(w, np.float32).astype(ml_dtypes.bfloat16)).reshape(k // 32, 32, n)
    amax = np.abs(w).max(1)
    if fmt == "e4m3":
        byte = np.frexp(amax)[1] - 1 + 127 - 7
    else:
        mant, ex = np.frexp(amax / 6.0)
        byte = np.where(mant > 0.5, ex, ex - 1) + 127
    byte = np.clip(np.where(amax > 0, byte, 1), 1, 254)
    scaled = (w * np.exp2(127.0 - byte)[:, None, :]).reshape(k, n).astype(np.float32)
    by_word = np.ascontiguousarray(scaled.reshape(k // 512, 128, 4, n).transpose(0, 1, 3, 2))
    if fmt == "e4m3":
        words = by_word.astype(ml_dtypes.float8_e4m3fn).view(np.uint8)
    else:
        c = by_word.astype(ml_dtypes.float4_e2m1fn).view(np.uint8) & 0xF
        words = (c[..., 0::2] | (c[..., 1::2] << 4)).reshape(k // 512, 128, 2 * n)
    return np.ascontiguousarray(words), np.ascontiguousarray(byte.astype(np.uint8).reshape(k // 512, 16, n))


def unpack_weight(words, scales, fmt):
    g, _, n = scales.shape
    words = np.ascontiguousarray(words).reshape(g, 128, n, -1)
    if fmt == "e4m3":
        vals = words.view(ml_dtypes.float8_e4m3fn).astype(np.float64)
    else:
        nib = np.empty((g, 128, n, 4), np.uint8)
        nib[..., 0::2] = words & 0xF
        nib[..., 1::2] = words >> 4
        vals = E2M1[nib]
    vals = vals * np.repeat(np.exp2(scales.astype(np.float64) - 127.0), 8, axis=1)[..., None]
    return vals.transpose(0, 1, 3, 2).reshape(g * 512, n)


def bf(x):
    return np.asarray(x, np.float32).astype(ml_dtypes.bfloat16)


def planes(Y):
    r, m = Y.shape
    b = f64(bf(Y)).reshape(r // 32, 32, m)
    amax = np.abs(b).max(1)
    byte = np.clip(np.where(amax > 0, np.frexp(amax)[1] - 1 + 127 - 7, 1), 1, 254)
    codes = (b * np.exp2(127.0 - byte)[:, None, :]).reshape(r, m).astype(np.float32).astype(ml_dtypes.float8_e4m3fn).view(np.uint8)
    words = codes.reshape(r // 512, 128, 4, m).transpose(0, 1, 3, 2)
    return np.ascontiguousarray(words), np.ascontiguousarray(byte.astype(np.uint8).reshape(r // 512, 16, m))


K, T, C, J, I, L, N = 512, 1024, 1024, 1024, 512, 512, 512


def setup_inputs():
    n = np.random.standard_normal
    idx = np.random.randint(0, C, J)
    idx2 = np.random.permutation(T)[:I]
    fk = mx_kscale(K)
    fj = mx_kscale(J)
    fl = mx_kscale(L)
    xtp = pack_weight(n((K, T)) / fk[:, None], "e2m1")
    wcp = pack_weight(n((K, C)) * 1 / np.sqrt(K) * fk[:, None], "e4m3")
    wop = pack_weight(n((J, N)) * 1 / np.sqrt(J) / fj[:, None], "e2m1")
    skp = pack_weight(n((L, I)) / fl[:, None], "e4m3")
    wsp = pack_weight(n((L, N)) * 1 / np.sqrt(L) * fl[:, None], "e2m1")
    return {
        "xt_words": xtp[0],
        "xt_scales": xtp[1],
        "wc_words": wcp[0],
        "wc_scales": wcp[1],
        "fj": (np.random.uniform(0.5, 2.0, (J, 1)) * fj[:, None]).astype(np.float32),
        "wo_words": wop[0],
        "wo_scales": wop[1],
        "sk_words": skp[0],
        "sk_scales": skp[1],
        "ws_words": wsp[0],
        "ws_scales": wsp[1],
        "offs": striped(idx),
        "offs2": striped(idx2),
    }


def reference(xt_words, xt_scales, wc_words, wc_scales, fj, wo_words, wo_scales, sk_words, sk_scales, ws_words, ws_scales, offs, offs2):
    idx = unstriped(offs)
    idx2 = unstriped(offs2)
    xtu = unpack_weight(xt_words, xt_scales, "e2m1")
    wcu = unpack_weight(wc_words, wc_scales, "e4m3")
    wou = unpack_weight(wo_words, wo_scales, "e2m1")
    sku = unpack_weight(sk_words, sk_scales, "e4m3")
    wsu = unpack_weight(ws_words, ws_scales, "e2m1")
    z = xtu.T @ wcu
    zj = z[:, idx]
    zt = zj.T
    u = zt[:, idx2] * f64(fj)
    uq = mxq(u, 0, "e4m3")
    y = wou.T @ uq + wsu.T @ sku
    words, scales = planes(y)
    return y, words, scales

@@ -1,0 +1,273 @@
+from contextlib import ExitStack
+
+import concourse.mybir as mybir
+from concourse.masks import make_identity
+
+K, T, C, J, I, L, N = 512, 1024, 1024, 1024, 512, 512, 512
+FLOPS = 2 * (K * T * C + J * N * I + L * N * I)
+
+F32 = mybir.dt.float32
+BF16 = mybir.dt.bfloat16
+I32 = mybir.dt.int32
+U32 = mybir.dt.uint32
+U16 = mybir.dt.uint16
+U8 = mybir.dt.uint8
+FP8X4 = mybir.dt.float8_e4m3fn_x4
+FP4X4 = mybir.dt.float4_e2m1fn_x4
+COPY = mybir.ActivationFunctionType.Copy
+MULT = mybir.AluOpType.mult
+
+P = 128
+PACK = 4
+PASS = P * PACK
+BANK = 512
+PER_COL = 16
+T_TILES = T // P
+J_PASSES = J // PASS
+XT_FIRST = 2
+AHEAD = 2
+ON_SCALAR = (5, 1)
+CHUNKS = ((0, 256), (256, 128), (384, 128))
+
+
+def load_scales(queue, plane, rows, quads=range(4)):
+    for quad in quads:
+        queue.dma_start(
+            out=plane[32 * quad : 32 * quad + 4].bitcast(I32),
+            in_=rows[:, 4 * quad : 4 * quad + 4, :].rearrange("g r n -> r g n").bitcast(I32),
+        )
+
+
+def tile_list_rows_then_columns_pl_kernel(
+    tc, xt_words, xt_scales, wc_words, wc_scales, fj, wo_words, wo_scales,
+    sk_words, sk_scales, ws_words, ws_scales, offs, offs2, out_0, out_1, out_2,
+):
+    nc = tc.nc
+    with ExitStack() as ctx:
+        lists = ctx.enter_context(tc.tile_pool(name="lists", bufs=1))
+        keep = ctx.enter_context(tc.tile_pool(name="keep", bufs=1))
+        ring = ctx.enter_context(tc.tile_pool(name="ring", bufs=4))
+        psum = ctx.enter_context(tc.psum_pool(name="psum", bufs=4))
+
+        offs_sb = lists.tile([P, J // PER_COL], U16, name="offs_sb")
+        offs2_sb = lists.tile([P, I // PER_COL], U16, name="offs2_sb")
+
+        xt_a = keep.tile([P, 2 * P * XT_FIRST], U8, name="xt_a", align_bytes=64)
+        xt_b = keep.tile([P, 2 * (T - P * XT_FIRST)], U8, name="xt_b", align_bytes=64)
+        wc_sb = keep.tile([P, C], U32, name="wc_sb", align_bytes=64)
+        xt_sc = keep.tile([P, 1, T], U8, name="xt_sc", align_bytes=64)
+        wc_sc = keep.tile([P, 1, C], U8, name="wc_sc", align_bytes=64)
+        w_raw = keep.tile([P, 3, 2 * N], U8, name="w_raw", align_bytes=64)
+        w_sc_raw = keep.tile([P, 3, N], U8, name="w_sc_raw", align_bytes=64)
+        w_sb = keep.tile([P, 3, 2 * N], U8, name="w_sb", align_bytes=64)
+        w_sc = keep.tile([P, 3, N], U8, name="w_sc", align_bytes=64)
+        sk_sb = keep.tile([P, I], U32, name="sk_sb", align_bytes=64)
+        sk_sc = keep.tile([P, 1, I], U8, name="sk_sc", align_bytes=64)
+        fj_sb = keep.tile([P, J_PASSES, PACK], F32, name="fj_sb")
+        ident = keep.tile([P, P], F32, name="ident", align_bytes=64)
+
+        nc.vector.memset(w_sc_raw[:].bitcast(U32), 0)
+
+        load_scales(nc.sync, xt_sc, xt_scales, range(0, 2))
+        load_scales(nc.scalar, wc_sc, wc_scales)
+        nc.sync.dma_start(out=wc_sb[:].bitcast(I32), in_=wc_words[0].rearrange("p n t -> p (n t)").bitcast(I32))
+        nc.sync.dma_start(out=xt_a[:].bitcast(I32), in_=xt_words[0, :, 0 : 2 * P * XT_FIRST].bitcast(I32))
+        load_scales(nc.sync, xt_sc, xt_scales, range(2, 4))
+        nc.sync.dma_start(offs_sb[:], offs)
+        nc.sync.dma_start(out=xt_b[:].bitcast(I32), in_=xt_words[0, :, 2 * P * XT_FIRST :].bitcast(I32))
+        load_scales(nc.sync, w_sc_raw[:, 0:2, :], wo_scales)
+        load_scales(nc.sync, w_sc_raw[:, 2:3, :], ws_scales)
+        nc.sync.dma_start(out=w_raw[:, 0:2, :].bitcast(I32), in_=wo_words.rearrange("g p b -> p g b").bitcast(I32))
+        nc.sync.dma_start(out=w_raw[:, 2, :].bitcast(I32), in_=ws_words[0].bitcast(I32))
+        nc.sync.dma_start(offs2_sb[:], offs2)
+        nc.sync.dma_start(out=fj_sb[:], in_=fj.rearrange("(g p t) o -> p g (t o)", g=J_PASSES, t=PACK))
+        load_scales(nc.sync, sk_sc, sk_scales)
+        nc.sync.dma_start(out=sk_sb[:].bitcast(I32), in_=sk_words[0].rearrange("p n t -> p (n t)").bitcast(I32))
+        make_identity(nc, ident[:])
+
+        z = [keep.tile([P, C], F32, name="z%d" % tt) for tt in range(T_TILES)]
+        zt = [keep.tile([P, PACK, T], F32, name="zt%d" % g) for g in range(J_PASSES)]
+
+        def make_z(tt):
+            if tt < XT_FIRST:
+                words = xt_a[:, 2 * P * tt : 2 * P * (tt + 1)]
+            else:
+                words = xt_b[:, 2 * P * (tt - XT_FIRST) : 2 * P * (tt - XT_FIRST + 1)]
+            for half in range(C // BANK):
+                cols = slice(half * BANK, (half + 1) * BANK)
+                acc = psum.tile([P, BANK], F32, name="acc", tag="sums")
+                nc.tensor.matmul_mx(
+                    out=acc[:], lhsT=words.bitcast(FP4X4), lhsT_scale=xt_sc[:, 0, P * tt : P * (tt + 1)],
+                    rhs=wc_sb[:, cols].bitcast(FP8X4), rhs_scale=wc_sc[:, 0, cols], start=True, stop=True,
+                )
+                if tt == 0 and half == 1:
+                    nc.vector.tensor_copy(out=z[tt][:, cols], in_=acc[:])
+                else:
+                    nc.scalar.copy(out=z[tt][:, cols], in_=acc[:])
+
+        def turn(tt, g):
+            zj = ring.tile([P, PACK, P], F32, name="zj")
+            cols = slice(g * PASS // PER_COL, (g + 1) * PASS // PER_COL)
+            window = z[tt][:].indirect(offs_sb[:, cols])
+            if (tt, g) == ON_SCALAR:
+                nc.scalar.activation(out=zj[:].rearrange("p t q -> p (t q)"), in_=window, func=COPY)
+                slots = zj[:].rearrange("p t q -> p (t q)").rearrange("p (q t) -> p t q", t=PACK)
+            else:
+                nc.vector.tensor_copy(out=zj[:].rearrange("p t q -> p q t"), in_=window)
+                slots = zj[:]
+            turned = psum.tile([P, PACK, P], F32, name="turned", tag="turned")
+            for t in range(PACK):
+                nc.tensor.transpose(turned[:, t, :], slots[:, t, :], ident[:])
+            nc.scalar.copy(out=zt[g][:, :, P * tt : P * (tt + 1)], in_=turned[:])
+
+        def deal_words():
+            nc.scalar.copy(
+                out=w_sb[:].bitcast(U16).rearrange("p a (t q) -> p a t q", t=PACK),
+                in_=w_raw[:].bitcast(U16).rearrange("p a (q t) -> p a t q", t=PACK),
+            )
+
+        def deal_scales():
+            for part in (slice(0, 2), slice(2, 3)):
+                nc.vector.tensor_copy(
+                    out=w_sc[:, part, :].rearrange("p a (t q) -> p a t q", t=PACK),
+                    in_=w_sc_raw[:, part, :].rearrange("p a (q t) -> p a t q", t=PACK),
+                )
+
+        for tt in range(AHEAD + 1):
+            make_z(tt)
+        for tt in range(T_TILES):
+            turn(tt, 0)
+            if tt < T_TILES - 1:
+                turn(tt, 1)
+            if tt + AHEAD + 1 < T_TILES:
+                make_z(tt + AHEAD + 1)
+            if tt == 2:
+                deal_scales()
+            if tt == T_TILES - AHEAD - 2:
+                deal_words()
+
+        y_scales = keep.tile([P, I], U8, name="y_scales", align_bytes=64)
+        out_rows = out_0.rearrange("(p t) i -> p t i", t=PACK)
+        out_words = out_1[0].rearrange("p c r -> p (c r)").bitcast(I32)
+
+        def product(bank, a, pair, codes, scales, start, stop):
+            for s in range(2):
+                t = 2 * pair + s
+                nc.tensor.matmul_mx(
+                    out=bank[:, s, :], lhsT=w_sb[:, a, 2 * P * t : 2 * P * (t + 1)].bitcast(FP4X4),
+                    lhsT_scale=w_sc[:, a, P * t : P * (t + 1)], rhs=codes.bitcast(FP8X4), rhs_scale=scales,
+                    start=start and s == 0, stop=stop and s == 1,
+                )
+
+        banks = {}
+
+        def skip(c):
+            i0, w = CHUNKS[c]
+            for pair in range(2):
+                banks[c, pair] = psum.tile([P, 2, w], F32, name="ybank", tag="sums" if c < 2 else "turned")
+                product(banks[c, pair], 2, pair, sk_sb[:, i0 : i0 + w], sk_sc[:, 0, i0 : i0 + w], True, False)
+
+        picked = {}
+        for c, (i0, w) in enumerate(CHUNKS):
+            for g in range(J_PASSES):
+                picked[c, g] = keep.tile([P, PACK, w], F32, name="picked%d_%d" % (c, g))
+
+        def pick(c, g, slots, on_vector):
+            i0, w = CHUNKS[c]
+            cols = slice(i0 // PER_COL, (i0 + w) // PER_COL)
+            for t in slots:
+                window = zt[g][:, t, :].indirect(offs2_sb[:, cols])
+                if on_vector:
+                    nc.vector.tensor_copy(out=picked[c, g][:, t, :], in_=window)
+                else:
+                    nc.scalar.activation(out=picked[c, g][:, t, :], in_=window, func=COPY)
+
+        u_bf = {}
+
+        def scale_u(c, g):
+            w = CHUNKS[c][1]
+            u_bf[c, g] = keep.tile([P, w * PACK], BF16, name="u_bf%d_%d" % (c, g), align_bytes=64)
+            nc.vector.tensor_tensor(
+                out=u_bf[c, g][:].rearrange("p (b i t) -> p b t i", i=4, t=PACK),
+                in0=picked[c, g][:].rearrange("p t (b i) -> p b t i", i=4),
+                in1=fj_sb[:, g, :].unsqueeze(1).unsqueeze(3).to_broadcast([P, w // 4, PACK, 4]),
+                op=MULT,
+            )
+
+        def multiply(c, g):
+            w = CHUNKS[c][1]
+            u_codes = keep.tile([P, w], U32, name="u_codes%d_%d" % (c, g), align_bytes=64)
+            u_scales = keep.tile([P, w], U8, name="u_scales%d_%d" % (c, g), align_bytes=64)
+            nc.vector.quantize_mx(out=u_codes[:].bitcast(FP8X4), scales=u_scales[:], in_=u_bf[c, g][:])
+            for pair in range(2):
+                product(banks[c, pair], g, pair, u_codes[:], u_scales[:], False, g == J_PASSES - 1)
+
+        y_sb = {}
+        y_bf = {}
+
+        def empty(c, vector_too):
+            i0, w = CHUNKS[c]
+            y_sb[c] = keep.tile([P, PACK, w], F32, name="y%d" % c)
+            if vector_too:
+                nc.vector.tensor_copy(out=y_sb[c][:, 0:2, :], in_=banks[c, 0][:])
+            else:
+                nc.scalar.copy(out=y_sb[c][:, 0:2, :], in_=banks[c, 0][:])
+            nc.scalar.copy(out=y_sb[c][:, 2:4, :], in_=banks[c, 1][:])
+            nc.sync.dma_start(out=out_rows[:, :, i0 : i0 + w], in_=y_sb[c][:])
+
+        def round_y(c):
+            w = CHUNKS[c][1]
+            y_bf[c] = keep.tile([P, w * PACK], BF16, name="y_bf%d" % c, align_bytes=64)
+            nc.vector.tensor_copy(
+                out=y_bf[c][:].rearrange("p (b i t) -> p b t i", i=4, t=PACK),
+                in_=y_sb[c][:].rearrange("p t (b i) -> p b t i", i=4),
+            )
+
+        def planes(c):
+            i0, w = CHUNKS[c]
+            y_codes = keep.tile([P, w], U32, name="y_codes%d" % c, align_bytes=64)
+            nc.vector.quantize_mx(out=y_codes[:].bitcast(FP8X4), scales=y_scales[:, i0 : i0 + w], in_=y_bf[c][:])
+            queue = nc.scalar if c == len(CHUNKS) - 1 else nc.sync
+            queue.dma_start(out=out_words[:, i0 : i0 + w], in_=y_codes[:].bitcast(I32))
+
+        skip(0)
+        skip(1)
+        pick(0, 0, (2,), False)
+        turn(T_TILES - 1, 1)
+        pick(0, 0, (0, 1), True)
+        pick(0, 0, (3,), False)
+        pick(0, 1, (0,), True)
+        pick(0, 1, (1, 2, 3), False)
+        skip(2)
+        scale_u(0, 0)
+        pick(1, 0, range(PACK), False)
+        multiply(0, 0)
+        scale_u(0, 1)
+        pick(1, 1, range(PACK), False)
+        multiply(0, 1)
+        scale_u(1, 0)
+        pick(2, 0, range(PACK), False)
+        multiply(1, 0)
+        scale_u(1, 1)
+        pick(2, 1, (0,), True)
+        pick(2, 1, (1, 2, 3), False)
+        multiply(1, 1)
+        empty(0, True)
+        scale_u(2, 0)
+        multiply(2, 0)
+        scale_u(2, 1)
+        round_y(0)
+        multiply(2, 1)
+        empty(1, False)
+        planes(0)
+        round_y(1)
+        empty(2, True)
+        planes(1)
+        round_y(2)
+        planes(2)
+        for quad in range(4):
+            queue = nc.sync if quad % 2 == 0 else nc.scalar
+            queue.dma_start(
+                out=out_2[0, 4 * quad : 4 * quad + 4, :].bitcast(I32),
+                in_=y_scales[32 * quad : 32 * quad + 4, :].bitcast(I32),
+            )

@@ -25,8 +25,8 @@ PER_COL = 16
 T_TILES = T // P
 J_PASSES = J // PASS
 XT_FIRST = 2
-AHEAD = 2
-ON_SCALAR = (5, 1)
+AHEAD = 4
+SPLIT = 1
 CHUNKS = ((0, 256), (256, 128), (384, 128))
 
 
@@ -46,7 +46,7 @@ def tile_list_rows_then_columns_pl_kernel(
     with ExitStack() as ctx:
         lists = ctx.enter_context(tc.tile_pool(name="lists", bufs=1))
         keep = ctx.enter_context(tc.tile_pool(name="keep", bufs=1))
-        ring = ctx.enter_context(tc.tile_pool(name="ring", bufs=4))
+        ring = ctx.enter_context(tc.tile_pool(name="ring", bufs=3))
         psum = ctx.enter_context(tc.psum_pool(name="psum", bufs=4))
 
         offs_sb = lists.tile([P, J // PER_COL], U16, name="offs_sb")
@@ -95,7 +95,7 @@ def tile_list_rows_then_columns_pl_kernel(
                 words = xt_b[:, 2 * P * (tt - XT_FIRST) : 2 * P * (tt - XT_FIRST + 1)]
             for half in range(C // BANK):
                 cols = slice(half * BANK, (half + 1) * BANK)
-                acc = psum.tile([P, BANK], F32, name="acc", tag="sums")
+                acc = psum.tile([P, BANK], F32, name="acc", tag="sums", bufs=5)
                 nc.tensor.matmul_mx(
                     out=acc[:], lhsT=words.bitcast(FP4X4), lhsT_scale=xt_sc[:, 0, P * tt : P * (tt + 1)],
                     rhs=wc_sb[:, cols].bitcast(FP8X4), rhs_scale=wc_sc[:, 0, cols], start=True, stop=True,
@@ -106,18 +106,12 @@ def tile_list_rows_then_columns_pl_kernel(
                     nc.scalar.copy(out=z[tt][:, cols], in_=acc[:])
 
         def turn(tt, g):
-            zj = ring.tile([P, PACK, P], F32, name="zj")
+            zj = ring.tile([P, 2, P, 2], F32, name="zj")
             cols = slice(g * PASS // PER_COL, (g + 1) * PASS // PER_COL)
-            window = z[tt][:].indirect(offs_sb[:, cols])
-            if (tt, g) == ON_SCALAR:
-                nc.scalar.activation(out=zj[:].rearrange("p t q -> p (t q)"), in_=window, func=COPY)
-                slots = zj[:].rearrange("p t q -> p (t q)").rearrange("p (q t) -> p t q", t=PACK)
-            else:
-                nc.vector.tensor_copy(out=zj[:].rearrange("p t q -> p q t"), in_=window)
-                slots = zj[:]
-            turned = psum.tile([P, PACK, P], F32, name="turned", tag="turned")
+            nc.vector.tensor_copy(out=zj[:].rearrange("p u q e -> p q u e"), in_=z[tt][:].indirect(offs_sb[:, cols]))
+            turned = psum.tile([P, PACK, P], F32, name="turned", tag="turned", bufs=3)
             for t in range(PACK):
-                nc.tensor.transpose(turned[:, t, :], slots[:, t, :], ident[:])
+                nc.tensor.transpose(turned[:, t, :], zj[:, t // 2, :, t % 2], ident[:])
             nc.scalar.copy(out=zt[g][:, :, P * tt : P * (tt + 1)], in_=turned[:])
 
         def deal_words():
@@ -137,13 +131,13 @@ def tile_list_rows_then_columns_pl_kernel(
             make_z(tt)
         for tt in range(T_TILES):
             turn(tt, 0)
-            if tt < T_TILES - 1:
+            if tt < SPLIT:
                 turn(tt, 1)
             if tt + AHEAD + 1 < T_TILES:
                 make_z(tt + AHEAD + 1)
             if tt == 2:
                 deal_scales()
-            if tt == T_TILES - AHEAD - 2:
+            if tt == 3:
                 deal_words()
 
         y_scales = keep.tile([P, I], U8, name="y_scales", align_bytes=64)
@@ -164,107 +158,107 @@ def tile_list_rows_then_columns_pl_kernel(
         def skip(c):
             i0, w = CHUNKS[c]
             for pair in range(2):
-                banks[c, pair] = psum.tile([P, 2, w], F32, name="ybank", tag="sums" if c < 2 else "turned")
+                banks[c, pair] = psum.tile([P, 2, w], F32, name="ybank", tag="sums" if 2 * c + pair < 5 else "turned", bufs=5 if 2 * c + pair < 5 else 3)
                 product(banks[c, pair], 2, pair, sk_sb[:, i0 : i0 + w], sk_sc[:, 0, i0 : i0 + w], True, False)
 
         picked = {}
-        for c, (i0, w) in enumerate(CHUNKS):
-            for g in range(J_PASSES):
-                picked[c, g] = keep.tile([P, PACK, w], F32, name="picked%d_%d" % (c, g))
+        u_bf = {}
 
-        def pick(c, g, slots, on_vector):
-            i0, w = CHUNKS[c]
+        def pick(g, span, slots, on_vector):
+            i0, w = span
+            if (g, span) not in picked:
+                picked[g, span] = keep.tile([P, PACK, w], F32, name="picked%d_%d" % (g, i0))
             cols = slice(i0 // PER_COL, (i0 + w) // PER_COL)
             for t in slots:
                 window = zt[g][:, t, :].indirect(offs2_sb[:, cols])
                 if on_vector:
-                    nc.vector.tensor_copy(out=picked[c, g][:, t, :], in_=window)
+                    nc.vector.tensor_copy(out=picked[g, span][:, t, :], in_=window)
                 else:
-                    nc.scalar.activation(out=picked[c, g][:, t, :], in_=window, func=COPY)
+                    nc.scalar.activation(out=picked[g, span][:, t, :], in_=window, func=COPY)
 
-        u_bf = {}
-
-        def scale_u(c, g):
-            w = CHUNKS[c][1]
-            u_bf[c, g] = keep.tile([P, w * PACK], BF16, name="u_bf%d_%d" % (c, g), align_bytes=64)
+        def scale_u(g, span):
+            i0, w = span
+            u_bf[g, span] = keep.tile([P, w * PACK], BF16, name="u_bf", align_bytes=64, bufs=1)
             nc.vector.tensor_tensor(
-                out=u_bf[c, g][:].rearrange("p (b i t) -> p b t i", i=4, t=PACK),
-                in0=picked[c, g][:].rearrange("p t (b i) -> p b t i", i=4),
+                out=u_bf[g, span][:].rearrange("p (b i t) -> p b t i", i=4, t=PACK),
+                in0=picked[g, span][:].rearrange("p t (b i) -> p b t i", i=4),
                 in1=fj_sb[:, g, :].unsqueeze(1).unsqueeze(3).to_broadcast([P, w // 4, PACK, 4]),
                 op=MULT,
             )
 
-        def multiply(c, g):
-            w = CHUNKS[c][1]
-            u_codes = keep.tile([P, w], U32, name="u_codes%d_%d" % (c, g), align_bytes=64)
-            u_scales = keep.tile([P, w], U8, name="u_scales%d_%d" % (c, g), align_bytes=64)
-            nc.vector.quantize_mx(out=u_codes[:].bitcast(FP8X4), scales=u_scales[:], in_=u_bf[c, g][:])
-            for pair in range(2):
-                product(banks[c, pair], g, pair, u_codes[:], u_scales[:], False, g == J_PASSES - 1)
+        def multiply(g, span):
+            s0, sw = span
+            u_codes = keep.tile([P, sw], U32, name="u_codes%d_%d" % (g, s0), align_bytes=64)
+            u_scales = keep.tile([P, sw], U8, name="u_scales%d_%d" % (g, s0), align_bytes=64)
+            nc.vector.quantize_mx(out=u_codes[:].bitcast(FP8X4), scales=u_scales[:], in_=u_bf[g, span][:])
+            for c, (i0, w) in enumerate(CHUNKS):
+                if s0 <= i0 < s0 + sw:
+                    cols = slice(i0 - s0, i0 - s0 + w)
+                    for pair in range(2):
+                        product(banks[c, pair], g, pair, u_codes[:, cols], u_scales[:, cols], False, g == J_PASSES - 1)
 
-        y_sb = {}
-        y_bf = {}
+        halves = ((0, 256), (256, 256))
+        y_sb = [keep.tile([P, PACK, w], F32, name="y%d" % i0) for i0, w in halves]
+        y_bf = [keep.tile([P, w * PACK], BF16, name="y_bf%d" % i0, align_bytes=64) for i0, w in halves]
 
-        def empty(c, vector_too):
+        def empty(c):
             i0, w = CHUNKS[c]
-            y_sb[c] = keep.tile([P, PACK, w], F32, name="y%d" % c)
-            if vector_too:
-                nc.vector.tensor_copy(out=y_sb[c][:, 0:2, :], in_=banks[c, 0][:])
-            else:
-                nc.scalar.copy(out=y_sb[c][:, 0:2, :], in_=banks[c, 0][:])
-            nc.scalar.copy(out=y_sb[c][:, 2:4, :], in_=banks[c, 1][:])
-            nc.sync.dma_start(out=out_rows[:, :, i0 : i0 + w], in_=y_sb[c][:])
+            h, at = divmod(i0, 256)
+            for pair in range(2):
+                nc.scalar.copy(out=y_sb[h][:, 2 * pair : 2 * pair + 2, at : at + w], in_=banks[c, pair][:])
+            if at + w == 256:
+                nc.sync.dma_start(out=out_rows[:, :, 256 * h : 256 * (h + 1)], in_=y_sb[h][:])
 
         def round_y(c):
-            w = CHUNKS[c][1]
-            y_bf[c] = keep.tile([P, w * PACK], BF16, name="y_bf%d" % c, align_bytes=64)
+            i0, w = CHUNKS[c]
+            h, at = divmod(i0, 256)
             nc.vector.tensor_copy(
-                out=y_bf[c][:].rearrange("p (b i t) -> p b t i", i=4, t=PACK),
-                in_=y_sb[c][:].rearrange("p t (b i) -> p b t i", i=4),
+                out=y_bf[h][:, PACK * at : PACK * (at + w)].rearrange("p (b i t) -> p b t i", i=4, t=PACK),
+                in_=y_sb[h][:, :, at : at + w].rearrange("p t (b i) -> p b t i", i=4),
             )
 
-        def planes(c):
-            i0, w = CHUNKS[c]
-            y_codes = keep.tile([P, w], U32, name="y_codes%d" % c, align_bytes=64)
-            nc.vector.quantize_mx(out=y_codes[:].bitcast(FP8X4), scales=y_scales[:, i0 : i0 + w], in_=y_bf[c][:])
-            queue = nc.scalar if c == len(CHUNKS) - 1 else nc.sync
+        def planes(h):
+            i0, w = halves[h]
+            y_codes = keep.tile([P, w], U32, name="y_codes%d" % h, align_bytes=64)
+            nc.vector.quantize_mx(out=y_codes[:].bitcast(FP8X4), scales=y_scales[:, i0 : i0 + w], in_=y_bf[h][:])
+            queue = nc.scalar if h == 1 else nc.sync
             queue.dma_start(out=out_words[:, i0 : i0 + w], in_=y_codes[:].bitcast(I32))
 
+        first, second = (0, 256), (256, 256)
+        early = [(span, t) for span in (first, second) for t in range(PACK)][:6]
+        late_tiles = list(range(SPLIT, T_TILES))
+        for n, tt in enumerate(late_tiles):
+            lo, hi = n * len(early) // len(late_tiles), (n + 1) * len(early) // len(late_tiles)
+            for span, t in early[lo:hi]:
+                pick(0, span, (t,), False)
+            turn(tt, 1)
         skip(0)
         skip(1)
-        pick(0, 0, (2,), False)
-        turn(T_TILES - 1, 1)
-        pick(0, 0, (0, 1), True)
-        pick(0, 0, (3,), False)
-        pick(0, 1, (0,), True)
-        pick(0, 1, (1, 2, 3), False)
         skip(2)
-        scale_u(0, 0)
-        pick(1, 0, range(PACK), False)
-        multiply(0, 0)
-        scale_u(0, 1)
-        pick(1, 1, range(PACK), False)
-        multiply(0, 1)
-        scale_u(1, 0)
-        pick(2, 0, range(PACK), False)
-        multiply(1, 0)
-        scale_u(1, 1)
-        pick(2, 1, (0,), True)
-        pick(2, 1, (1, 2, 3), False)
-        multiply(1, 1)
-        empty(0, True)
-        scale_u(2, 0)
-        multiply(2, 0)
-        scale_u(2, 1)
+        scale_u(0, first)
+        pick(0, second, range(6 - PACK, PACK), True)
+        multiply(0, first)
+        scale_u(0, second)
+        pick(1, CHUNKS[0], range(1), True)
+        multiply(0, second)
+        pick(1, CHUNKS[0], range(1, PACK), False)
+        scale_u(1, CHUNKS[0])
+        pick(1, CHUNKS[1], range(PACK), False)
+        multiply(1, CHUNKS[0])
+        scale_u(1, CHUNKS[1])
+        empty(0)
+        multiply(1, CHUNKS[1])
+        pick(1, CHUNKS[2], range(0), True)
+        pick(1, CHUNKS[2], range(0, PACK), False)
         round_y(0)
-        multiply(2, 1)
-        empty(1, False)
+        scale_u(1, CHUNKS[2])
         planes(0)
+        multiply(1, CHUNKS[2])
+        empty(1)
         round_y(1)
-        empty(2, True)
-        planes(1)
+        empty(2)
         round_y(2)
-        planes(2)
+        planes(1)
         for quad in range(4):
             queue = nc.sync if quad % 2 == 0 else nc.scalar
             queue.dma_start(

@@ -25,8 +25,9 @@ PER_COL = 16
 T_TILES = T // P
 J_PASSES = J // PASS
 XT_FIRST = 2
+DEALT_TURNS = 4
 AHEAD = 4
-SPLIT = 1
+SPLIT = 2
 CHUNKS = ((0, 256), (256, 128), (384, 128))
 
 
@@ -105,13 +106,23 @@ def tile_list_rows_then_columns_pl_kernel(
                 else:
                     nc.scalar.copy(out=z[tt][:, cols], in_=acc[:])
 
+        turns = []
+
         def turn(tt, g):
-            zj = ring.tile([P, 2, P, 2], F32, name="zj")
+            zj = ring.tile([P, PACK, P], F32, name="zj")
             cols = slice(g * PASS // PER_COL, (g + 1) * PASS // PER_COL)
-            nc.vector.tensor_copy(out=zj[:].rearrange("p u q e -> p q u e"), in_=z[tt][:].indirect(offs_sb[:, cols]))
+            window = z[tt][:].indirect(offs_sb[:, cols])
+            if len(turns) < DEALT_TURNS:
+                nc.vector.tensor_copy(out=zj[:].rearrange("p t q -> p q t"), in_=window)
+                slots = zj[:]
+            else:
+                in_order = zj[:].rearrange("p t q -> p (t q)")
+                nc.vector.tensor_copy(out=in_order, in_=window)
+                slots = in_order.rearrange("p (q t) -> p t q", t=PACK)
+            turns.append((tt, g))
             turned = psum.tile([P, PACK, P], F32, name="turned", tag="turned", bufs=3)
             for t in range(PACK):
-                nc.tensor.transpose(turned[:, t, :], zj[:, t // 2, :, t % 2], ident[:])
+                nc.tensor.transpose(turned[:, t, :], slots[:, t, :], ident[:])
             nc.scalar.copy(out=zt[g][:, :, P * tt : P * (tt + 1)], in_=turned[:])
 
         def deal_words():

from contextlib import ExitStack

import concourse.mybir as mybir
from concourse.masks import make_identity

K, T, C, J, I, L, N = 512, 1024, 1024, 1024, 512, 512, 512
FLOPS = 2 * (K * T * C + J * N * I + L * N * I)

F32 = mybir.dt.float32
BF16 = mybir.dt.bfloat16
I32 = mybir.dt.int32
U32 = mybir.dt.uint32
U16 = mybir.dt.uint16
U8 = mybir.dt.uint8
FP8X4 = mybir.dt.float8_e4m3fn_x4
FP4X4 = mybir.dt.float4_e2m1fn_x4
COPY = mybir.ActivationFunctionType.Copy
MULT = mybir.AluOpType.mult

P = 128
PACK = 4
PASS = P * PACK
BANK = 512
PER_COL = 16
T_TILES = T // P
J_PASSES = J // PASS
XT_FIRST = 2
DEALT_TURNS = 4
AHEAD = 4
SPLIT = 2
CHUNKS = ((0, 256), (256, 128), (384, 128))


def load_scales(queue, plane, rows, quads=range(4)):
    for quad in quads:
        queue.dma_start(
            out=plane[32 * quad : 32 * quad + 4].bitcast(I32),
            in_=rows[:, 4 * quad : 4 * quad + 4, :].rearrange("g r n -> r g n").bitcast(I32),
        )


def tile_list_rows_then_columns_pl_kernel(
    tc, xt_words, xt_scales, wc_words, wc_scales, fj, wo_words, wo_scales,
    sk_words, sk_scales, ws_words, ws_scales, offs, offs2, out_0, out_1, out_2,
):
    nc = tc.nc
    with ExitStack() as ctx:
        lists = ctx.enter_context(tc.tile_pool(name="lists", bufs=1))
        keep = ctx.enter_context(tc.tile_pool(name="keep", bufs=1))
        ring = ctx.enter_context(tc.tile_pool(name="ring", bufs=3))
        psum = ctx.enter_context(tc.psum_pool(name="psum", bufs=4))

        offs_sb = lists.tile([P, J // PER_COL], U16, name="offs_sb")
        offs2_sb = lists.tile([P, I // PER_COL], U16, name="offs2_sb")

        xt_a = keep.tile([P, 2 * P * XT_FIRST], U8, name="xt_a", align_bytes=64)
        xt_b = keep.tile([P, 2 * (T - P * XT_FIRST)], U8, name="xt_b", align_bytes=64)
        wc_sb = keep.tile([P, C], U32, name="wc_sb", align_bytes=64)
        xt_sc = keep.tile([P, 1, T], U8, name="xt_sc", align_bytes=64)
        wc_sc = keep.tile([P, 1, C], U8, name="wc_sc", align_bytes=64)
        w_raw = keep.tile([P, 3, 2 * N], U8, name="w_raw", align_bytes=64)
        w_sc_raw = keep.tile([P, 3, N], U8, name="w_sc_raw", align_bytes=64)
        w_sb = keep.tile([P, 3, 2 * N], U8, name="w_sb", align_bytes=64)
        w_sc = keep.tile([P, 3, N], U8, name="w_sc", align_bytes=64)
        sk_sb = keep.tile([P, I], U32, name="sk_sb", align_bytes=64)
        sk_sc = keep.tile([P, 1, I], U8, name="sk_sc", align_bytes=64)
        fj_sb = keep.tile([P, J_PASSES, PACK], F32, name="fj_sb")
        ident = keep.tile([P, P], F32, name="ident", align_bytes=64)

        nc.vector.memset(w_sc_raw[:].bitcast(U32), 0)

        load_scales(nc.sync, xt_sc, xt_scales, range(0, 2))
        load_scales(nc.scalar, wc_sc, wc_scales)
        nc.sync.dma_start(out=wc_sb[:].bitcast(I32), in_=wc_words[0].rearrange("p n t -> p (n t)").bitcast(I32))
        nc.sync.dma_start(out=xt_a[:].bitcast(I32), in_=xt_words[0, :, 0 : 2 * P * XT_FIRST].bitcast(I32))
        load_scales(nc.sync, xt_sc, xt_scales, range(2, 4))
        nc.sync.dma_start(offs_sb[:], offs)
        nc.sync.dma_start(out=xt_b[:].bitcast(I32), in_=xt_words[0, :, 2 * P * XT_FIRST :].bitcast(I32))
        load_scales(nc.sync, w_sc_raw[:, 0:2, :], wo_scales)
        load_scales(nc.sync, w_sc_raw[:, 2:3, :], ws_scales)
        nc.sync.dma_start(out=w_raw[:, 0:2, :].bitcast(I32), in_=wo_words.rearrange("g p b -> p g b").bitcast(I32))
        nc.sync.dma_start(out=w_raw[:, 2, :].bitcast(I32), in_=ws_words[0].bitcast(I32))
        nc.sync.dma_start(offs2_sb[:], offs2)
        nc.sync.dma_start(out=fj_sb[:], in_=fj.rearrange("(g p t) o -> p g (t o)", g=J_PASSES, t=PACK))
        load_scales(nc.sync, sk_sc, sk_scales)
        nc.sync.dma_start(out=sk_sb[:].bitcast(I32), in_=sk_words[0].rearrange("p n t -> p (n t)").bitcast(I32))
        make_identity(nc, ident[:])

        z = [keep.tile([P, C], F32, name="z%d" % tt) for tt in range(T_TILES)]
        zt = [keep.tile([P, PACK, T], F32, name="zt%d" % g) for g in range(J_PASSES)]

        def make_z(tt):
            if tt < XT_FIRST:
                words = xt_a[:, 2 * P * tt : 2 * P * (tt + 1)]
            else:
                words = xt_b[:, 2 * P * (tt - XT_FIRST) : 2 * P * (tt - XT_FIRST + 1)]
            for half in range(C // BANK):
                cols = slice(half * BANK, (half + 1) * BANK)
                acc = psum.tile([P, BANK], F32, name="acc", tag="sums", bufs=5)
                nc.tensor.matmul_mx(
                    out=acc[:], lhsT=words.bitcast(FP4X4), lhsT_scale=xt_sc[:, 0, P * tt : P * (tt + 1)],
                    rhs=wc_sb[:, cols].bitcast(FP8X4), rhs_scale=wc_sc[:, 0, cols], start=True, stop=True,
                )
                if tt == 0 and half == 1:
                    nc.vector.tensor_copy(out=z[tt][:, cols], in_=acc[:])
                else:
                    nc.scalar.copy(out=z[tt][:, cols], in_=acc[:])

        turns = []

        def turn(tt, g):
            zj = ring.tile([P, PACK, P], F32, name="zj")
            cols = slice(g * PASS // PER_COL, (g + 1) * PASS // PER_COL)
            window = z[tt][:].indirect(offs_sb[:, cols])
            if len(turns) < DEALT_TURNS:
                nc.vector.tensor_copy(out=zj[:].rearrange("p t q -> p q t"), in_=window)
                slots = zj[:]
            else:
                in_order = zj[:].rearrange("p t q -> p (t q)")
                nc.vector.tensor_copy(out=in_order, in_=window)
                slots = in_order.rearrange("p (q t) -> p t q", t=PACK)
            turns.append((tt, g))
            turned = psum.tile([P, PACK, P], F32, name="turned", tag="turned", bufs=3)
            for t in range(PACK):
                nc.tensor.transpose(turned[:, t, :], slots[:, t, :], ident[:])
            nc.scalar.copy(out=zt[g][:, :, P * tt : P * (tt + 1)], in_=turned[:])

        def deal_words():
            nc.scalar.copy(
                out=w_sb[:].bitcast(U16).rearrange("p a (t q) -> p a t q", t=PACK),
                in_=w_raw[:].bitcast(U16).rearrange("p a (q t) -> p a t q", t=PACK),
            )

        def deal_scales():
            for part in (slice(0, 2), slice(2, 3)):
                nc.vector.tensor_copy(
                    out=w_sc[:, part, :].rearrange("p a (t q) -> p a t q", t=PACK),
                    in_=w_sc_raw[:, part, :].rearrange("p a (q t) -> p a t q", t=PACK),
                )

        for tt in range(AHEAD + 1):
            make_z(tt)
        for tt in range(T_TILES):
            turn(tt, 0)
            if tt < SPLIT:
                turn(tt, 1)
            if tt + AHEAD + 1 < T_TILES:
                make_z(tt + AHEAD + 1)
            if tt == 2:
                deal_scales()
            if tt == 3:
                deal_words()

        y_scales = keep.tile([P, I], U8, name="y_scales", align_bytes=64)
        out_rows = out_0.rearrange("(p t) i -> p t i", t=PACK)
        out_words = out_1[0].rearrange("p c r -> p (c r)").bitcast(I32)

        def product(bank, a, pair, codes, scales, start, stop):
            for s in range(2):
                t = 2 * pair + s
                nc.tensor.matmul_mx(
                    out=bank[:, s, :], lhsT=w_sb[:, a, 2 * P * t : 2 * P * (t + 1)].bitcast(FP4X4),
                    lhsT_scale=w_sc[:, a, P * t : P * (t + 1)], rhs=codes.bitcast(FP8X4), rhs_scale=scales,
                    start=start and s == 0, stop=stop and s == 1,
                )

        banks = {}

        def skip(c):
            i0, w = CHUNKS[c]
            for pair in range(2):
                banks[c, pair] = psum.tile([P, 2, w], F32, name="ybank", tag="sums" if 2 * c + pair < 5 else "turned", bufs=5 if 2 * c + pair < 5 else 3)
                product(banks[c, pair], 2, pair, sk_sb[:, i0 : i0 + w], sk_sc[:, 0, i0 : i0 + w], True, False)

        picked = {}
        u_bf = {}

        def pick(g, span, slots, on_vector):
            i0, w = span
            if (g, span) not in picked:
                picked[g, span] = keep.tile([P, PACK, w], F32, name="picked%d_%d" % (g, i0))
            cols = slice(i0 // PER_COL, (i0 + w) // PER_COL)
            for t in slots:
                window = zt[g][:, t, :].indirect(offs2_sb[:, cols])
                if on_vector:
                    nc.vector.tensor_copy(out=picked[g, span][:, t, :], in_=window)
                else:
                    nc.scalar.activation(out=picked[g, span][:, t, :], in_=window, func=COPY)

        def scale_u(g, span):
            i0, w = span
            u_bf[g, span] = keep.tile([P, w * PACK], BF16, name="u_bf", align_bytes=64, bufs=1)
            nc.vector.tensor_tensor(
                out=u_bf[g, span][:].rearrange("p (b i t) -> p b t i", i=4, t=PACK),
                in0=picked[g, span][:].rearrange("p t (b i) -> p b t i", i=4),
                in1=fj_sb[:, g, :].unsqueeze(1).unsqueeze(3).to_broadcast([P, w // 4, PACK, 4]),
                op=MULT,
            )

        def multiply(g, span):
            s0, sw = span
            u_codes = keep.tile([P, sw], U32, name="u_codes%d_%d" % (g, s0), align_bytes=64)
            u_scales = keep.tile([P, sw], U8, name="u_scales%d_%d" % (g, s0), align_bytes=64)
            nc.vector.quantize_mx(out=u_codes[:].bitcast(FP8X4), scales=u_scales[:], in_=u_bf[g, span][:])
            for c, (i0, w) in enumerate(CHUNKS):
                if s0 <= i0 < s0 + sw:
                    cols = slice(i0 - s0, i0 - s0 + w)
                    for pair in range(2):
                        product(banks[c, pair], g, pair, u_codes[:, cols], u_scales[:, cols], False, g == J_PASSES - 1)

        halves = ((0, 256), (256, 256))
        y_sb = [keep.tile([P, PACK, w], F32, name="y%d" % i0) for i0, w in halves]
        y_bf = [keep.tile([P, w * PACK], BF16, name="y_bf%d" % i0, align_bytes=64) for i0, w in halves]

        def empty(c):
            i0, w = CHUNKS[c]
            h, at = divmod(i0, 256)
            for pair in range(2):
                nc.scalar.copy(out=y_sb[h][:, 2 * pair : 2 * pair + 2, at : at + w], in_=banks[c, pair][:])
            if at + w == 256:
                nc.sync.dma_start(out=out_rows[:, :, 256 * h : 256 * (h + 1)], in_=y_sb[h][:])

        def round_y(c):
            i0, w = CHUNKS[c]
            h, at = divmod(i0, 256)
            nc.vector.tensor_copy(
                out=y_bf[h][:, PACK * at : PACK * (at + w)].rearrange("p (b i t) -> p b t i", i=4, t=PACK),
                in_=y_sb[h][:, :, at : at + w].rearrange("p t (b i) -> p b t i", i=4),
            )

        def planes(h):
            i0, w = halves[h]
            y_codes = keep.tile([P, w], U32, name="y_codes%d" % h, align_bytes=64)
            nc.vector.quantize_mx(out=y_codes[:].bitcast(FP8X4), scales=y_scales[:, i0 : i0 + w], in_=y_bf[h][:])
            queue = nc.scalar if h == 1 else nc.sync
            queue.dma_start(out=out_words[:, i0 : i0 + w], in_=y_codes[:].bitcast(I32))

        first, second = (0, 256), (256, 256)
        early = [(span, t) for span in (first, second) for t in range(PACK)][:6]
        late_tiles = list(range(SPLIT, T_TILES))
        for n, tt in enumerate(late_tiles):
            lo, hi = n * len(early) // len(late_tiles), (n + 1) * len(early) // len(late_tiles)
            for span, t in early[lo:hi]:
                pick(0, span, (t,), False)
            turn(tt, 1)
        skip(0)
        skip(1)
        skip(2)
        scale_u(0, first)
        pick(0, second, range(6 - PACK, PACK), True)
        multiply(0, first)
        scale_u(0, second)
        pick(1, CHUNKS[0], range(1), True)
        multiply(0, second)
        pick(1, CHUNKS[0], range(1, PACK), False)
        scale_u(1, CHUNKS[0])
        pick(1, CHUNKS[1], range(PACK), False)
        multiply(1, CHUNKS[0])
        scale_u(1, CHUNKS[1])
        empty(0)
        multiply(1, CHUNKS[1])
        pick(1, CHUNKS[2], range(0), True)
        pick(1, CHUNKS[2], range(0, PACK), False)
        round_y(0)
        scale_u(1, CHUNKS[2])
        planes(0)
        multiply(1, CHUNKS[2])
        empty(1)
        round_y(1)
        empty(2)
        round_y(2)
        planes(1)
        for quad in range(4):
            queue = nc.sync if quad % 2 == 0 else nc.scalar
            queue.dma_start(
                out=out_2[0, 4 * quad : 4 * quad + 4, :].bitcast(I32),
                in_=y_scales[32 * quad : 32 * quad + 4, :].bitcast(I32),
            )
